import numpy as np
import ml_dtypes


def mxq(x, axis, fmt="e4m3"):
    dtype, down = {"e4m3": (ml_dtypes.float8_e4m3fn, 7), "e5m2": (ml_dtypes.float8_e5m2, 14)}[fmt]
    v = np.moveaxis(np.asarray(x, np.float32).astype(ml_dtypes.bfloat16).astype(np.float64), axis, -1)
    blocks = v.reshape(v.shape[:-1] + (-1, 32))
    amax = np.abs(blocks).max(-1, keepdims=True)
    byte = np.maximum(np.where(amax > 0, np.frexp(amax)[1] - 1 + 127, 0) - down, 1)
    scale = np.exp2(byte - 127.0)
    codes = (blocks / scale).astype(np.float32).astype(dtype).astype(np.float64)
    return np.moveaxis((codes * scale).reshape(v.shape), -1, axis)


WIDE = False


def mx_kscale(k):
    if not WIDE:
        return np.ones(k)
    levels = np.array([10, -10, 5, -5, 0])
    if k % 512:
        return np.exp2(np.random.permutation(np.resize(levels, k // 32))).repeat(32)
    a = np.empty((k // 512, 16))
    for p in range(k // 512):
        a[p, :8] = np.random.permutation(np.resize(levels, 8))
        for g in range(8):
            far = levels[np.abs(levels - a[p, g]) >= 10]
            a[p, g + 8] = far[np.random.randint(len(far))]
    return np.exp2(a.ravel()).repeat(32)


def f64(x):
    return np.asarray(x).astype(np.float64)


def striped(idx):
    return np.tile(np.asarray(idx).reshape(-1, 16).T, (8, 1)).astype(np.uint16)


def unstriped(offs):
    return offs[:16].T.reshape(-1).astype(np.int64)


E2M1 = np.array([0.0, 0.5, 1.0, 1.5, 2.0, 3.0, 4.0, 6.0, -0.0, -0.5, -1.0, -1.5, -2.0, -3.0, -4.0, -6.0])


def pack_weight(w, fmt):
    k, n = w.shape
    w = f64(np.asarray(w, np.float32).astype(ml_dtypes.bfloat16)).reshape(k // 32, 32, n)
    amax = np.abs(w).max(1)
    if fmt == "e4m3":
        byte = np.frexp(amax)[1] - 1 + 127 - 7
    else:
        mant, ex = np.frexp(amax / 6.0)
        byte = np.where(mant > 0.5, ex, ex - 1) + 127
    byte = np.clip(np.where(amax > 0, byte, 1), 1, 254)
    scaled = (w * np.exp2(127.0 - byte)[:, None, :]).reshape(k, n).astype(np.float32)
    by_word = np.ascontiguousarray(scaled.reshape(k // 512, 128, 4, n).transpose(0, 1, 3, 2))
    if fmt == "e4m3":
        words = by_word.astype(ml_dtypes.float8_e4m3fn).view(np.uint8)
    else:
        c = by_word.astype(ml_dtypes.float4_e2m1fn).view(np.uint8) & 0xF
        words = (c[..., 0::2] | (c[..., 1::2] << 4)).reshape(k // 512, 128, 2 * n)
    return np.ascontiguousarray(words), np.ascontiguousarray(byte.astype(np.uint8).reshape(k // 512, 16, n))


def unpack_weight(words, scales, fmt):
    g, _, n = scales.shape
    words = np.ascontiguousarray(words).reshape(g, 128, n, -1)
    if fmt == "e4m3":
        vals = words.view(ml_dtypes.float8_e4m3fn).astype(np.float64)
    else:
        nib = np.empty((g, 128, n, 4), np.uint8)
        nib[..., 0::2] = words & 0xF
        nib[..., 1::2] = words >> 4
        vals = E2M1[nib]
    vals = vals * np.repeat(np.exp2(scales.astype(np.float64) - 127.0), 8, axis=1)[..., None]
    return vals.transpose(0, 1, 3, 2).reshape(g * 512, n)


D, E, T, I, Q, G, U = 512, 512, 2048, 512, 128, 64, 256


def setup_inputs():
    n = np.random.standard_normal
    idx = np.random.permutation(T)[:I]
    idx2 = np.random.permutation(U)[:G]
    fd = mx_kscale(D)
    fe = mx_kscale(E)
    fi = mx_kscale(I)
    ti = np.ones(T)
    ti[idx] = fi
    keysp = pack_weight(n((D, T)) / fd[:, None], "e2m1")
    valsp = pack_weight(n((E, T)) / fe[:, None], "e2m1")
    return {
        "query": (n((D, Q)) * 1.0 / np.sqrt(D) * fd[:, None]).astype(np.float32),
        "keys_words": keysp[0],
        "keys_scales": keysp[1],
        "gout": (n((E, Q)) * 1 / np.sqrt(E) * fe[:, None]).astype(np.float32),
        "vals_words": valsp[0],
        "vals_scales": valsp[1],
        "pofs": (n((E, U)) / fe[:, None]).astype(np.float32),
        "pf": (np.random.uniform(0.5, 2.0, (Q, 1))).astype(np.float32),
        "fs": (np.random.uniform(128.0, 512.0, (1, I)) * fi).astype(np.float32),
        "keyrows": (n((D, T)) / ti).astype(np.float32),
        "res": (n((Q, D)) * 4.0).astype(np.float32),
        "offs": striped(idx),
        "offs2": striped(idx2),
    }


def reference(query, keys_words, keys_scales, gout, vals_words, vals_scales, pofs, pf, fs, keyrows, res, offs, offs2):
    idx = unstriped(offs)
    idx2 = unstriped(offs2)
    keysu = unpack_weight(keys_words, keys_scales, "e2m1")
    valsu = unpack_weight(vals_words, vals_scales, "e2m1")
    queryq = mxq(f64(query), 0, "e4m3")
    keysidxg = keysu[:, idx]
    a = queryq.T @ keysidxg
    p = np.exp(a - np.max(a, axis=1, keepdims=True))
    z = np.sum(p, axis=1, keepdims=True)
    s = p.reshape(Q, G, I // G).sum(axis=2) * f64(pf)
    goutq = mxq(f64(gout), 0, "e4m3")
    valsidxg = valsu[:, idx]
    c0 = goutq.T @ valsidxg
    pofsidx2q = mxq(f64(pofs)[:, idx2], 0, "e4m3")
    c1 = goutq.T @ pofsidx2q
    ds = 1.0 / z * c1
    e1 = ds * f64(pf)
    r1 = np.repeat(e1, I // G, axis=1)
    dz = (np.sum(p * c0, axis=1, keepdims=True) + np.sum(s * c1, axis=1, keepdims=True)) / np.square(z) * (-1.0)
    dp = 1.0 / z * c0 + r1 + dz
    da = dp * p
    gs = da * f64(fs)
    gt1 = gs.T
    kt = f64(keyrows)[:, idx].T
    gt1q = mxq(gt1, 0, "e4m3")
    ktq = mxq(kt, 0, "e4m3")
    gq = gt1q.T @ ktq
    y = gq + f64(res)
    return y

@@ -1,0 +1,168 @@
+from contextlib import ExitStack
+
+import concourse.mybir as mybir
+from concourse.masks import make_identity
+
+D, E, T, I, Q, G, U = 512, 512, 2048, 512, 128, 64, 256
+FLOPS = 2 * Q * (D * I + E * I + E * G + I * D)
+
+F32 = mybir.dt.float32
+BF16 = mybir.dt.bfloat16
+I32 = mybir.dt.int32
+U32 = mybir.dt.uint32
+U16 = mybir.dt.uint16
+U8 = mybir.dt.uint8
+FP8X4 = mybir.dt.float8_e4m3fn_x4
+FP4X4 = mybir.dt.float4_e2m1fn_x4
+ACT = mybir.ActivationFunctionType
+ALU = mybir.AluOpType
+AX = mybir.AxisListType
+
+P = 128
+PACK = 4
+DT = D // P
+PAGE = I // G
+
+
+def tile_attend_bpageoffsets_q_kernel(tc, query, keys_words, keys_scales, gout, vals_words, vals_scales,
+                                       pofs, pf, fs, keyrows, res, offs, offs2, out):
+    nc = tc.nc
+    with ExitStack() as ctx:
+        sb = ctx.enter_context(tc.tile_pool(name="sb", bufs=1))
+        ps = ctx.enter_context(tc.psum_pool(name="ps", bufs=1))
+
+        def tile(name, shape, dtype):
+            return sb.tile(shape, dtype, name=name, align_bytes=64)
+
+        def quantize(name, grouped, words):
+            codes = tile(name + "_codes", [P, words], U32)
+            scales = tile(name + "_scales", [P, words], U8)
+            nc.vector.quantize_mx(out=codes[:].bitcast(FP8X4), scales=scales[:], in_=grouped)
+            return codes, scales
+
+        idx = tile("idx", [P, I // 16], U16)
+        idx2 = tile("idx2", [P, G // 16], U16)
+        kw = tile("kw", [P, T], U16)
+        vw = tile("vw", [P, T], U16)
+        ks = tile("ks", [P, T], U8)
+        vs = tile("vs", [P, T], U8)
+        q_raw = tile("q_raw", [P, PACK, Q], F32)
+        g_raw = tile("g_raw", [P, PACK, Q], F32)
+        o_raw = tile("o_raw", [P, PACK * U], F32)
+        pf_sb = tile("pf_sb", [P, 1], F32)
+        fs_sb = tile("fs_sb", [P, PACK], F32)
+        kr = [tile("kr%d" % j, [P, T], F32) for j in range(DT)]
+        res_sb = tile("res_sb", [P, D], F32)
+        ident = tile("ident", [P, P], F32)
+        warm = tile("warm", [P, 1], F32)
+        warm_out = tile("warm_out", [P, 1], F32)
+        o_bf = tile("o_bf", [P, (PACK + 1) * U], BF16)
+
+        nc.vector.memset(ks[:].bitcast(I32), 0)
+        nc.vector.memset(vs[:].bitcast(I32), 0)
+        nc.vector.memset(warm[:], 0.0)
+        nc.vector.memset(o_bf[:, PACK * U:], 0.0)
+        make_identity(nc, ident[:])
+
+        nc.sync.dma_start(idx[:], offs)
+        nc.sync.dma_start(kw[:].bitcast(I32), keys_words[0].bitcast(I32))
+        for c in range(4):
+            nc.scalar.dma_start(ks[32 * c:32 * c + 4, :].bitcast(I32), keys_scales[0, 4 * c:4 * c + 4, :].bitcast(I32))
+        nc.scalar.activation(warm_out[:], warm[:], ACT.Exp)
+        nc.sync.dma_start(q_raw[:], query.rearrange("(p j) w -> p j w", j=PACK))
+        nc.sync.dma_start(o_raw[:], pofs.rearrange("(p j) w -> p (j w)", j=PACK))
+        nc.sync.dma_start(idx2[:], offs2)
+        nc.sync.dma_start(g_raw[:], gout.rearrange("(p j) w -> p j w", j=PACK))
+        nc.sync.dma_start(vw[:].bitcast(I32), vals_words[0].bitcast(I32))
+        for c in range(4):
+            nc.scalar.dma_start(vs[32 * c:32 * c + 4, :].bitcast(I32), vals_scales[0, 4 * c:4 * c + 4, :].bitcast(I32))
+        for j in range(DT):
+            nc.sync.dma_start(kr[j][:], keyrows[j * P:(j + 1) * P, :])
+        nc.sync.dma_start(res_sb[:], res)
+        nc.gpsimd.dma_start(pf_sb[:], pf)
+        nc.gpsimd.dma_start(fs_sb[:], fs.rearrange("o (p t) -> (o p) t", t=PACK))
+
+        kw_g = tile("kw_g", [P, I], U16)
+        ks_g = tile("ks_g", [P, I], U8)
+        nc.vector.tensor_copy(kw_g[:], kw[:].indirect(idx[:]))
+        q_bf = tile("q_bf", [P, Q, PACK], BF16)
+        nc.scalar.copy(q_bf[:], q_raw[:].rearrange("p j w -> p w j"))
+        nc.vector.tensor_copy(ks_g[:], ks[:].indirect(idx[:]))
+        q_codes, q_scales = quantize("q", q_bf[:].rearrange("p w j -> p (w j)"), Q)
+        a_ps = ps.tile([P, I], F32, name="a_ps")
+        nc.tensor.matmul_mx(out=a_ps[:], lhsT=q_codes[:].bitcast(FP8X4), lhsT_scale=q_scales[:],
+                            rhs=kw_g[:].bitcast(FP4X4), rhs_scale=ks_g[:], start=True, stop=True)
+
+        nc.scalar.copy(o_bf[:, :PACK * U], o_raw[:])
+        o_g = tile("o_g", [P, G, PACK], BF16)
+        for t in range(PACK):
+            nc.scalar.activation(o_g[:, :, t], o_bf[:, t * U:(t + 2) * U].indirect(idx2[:]), ACT.Copy)
+        g_bf = tile("g_bf", [P, Q, PACK], BF16)
+        nc.scalar.copy(g_bf[:], g_raw[:].rearrange("p j w -> p w j"))
+
+        neg_max = tile("neg_max", [P, 1], F32)
+        nc.vector.tensor_reduce(neg_max[:], a_ps[:], AX.X, ALU.max, negate=True)
+        p_sb = tile("p_sb", [P, PACK, P], F32)
+        z = tile("z", [P, 1], F32)
+        nc.scalar.activation(p_sb[:], a_ps[:].rearrange("q (p t) -> q t p", t=PACK), ACT.Exp,
+                             bias=neg_max[:], accum_out=z[:])
+
+        vw_g = tile("vw_g", [P, I], U16)
+        vs_g = tile("vs_g", [P, I], U8)
+        nc.vector.tensor_copy(vw_g[:], vw[:].indirect(idx[:]))
+        nc.vector.tensor_copy(vs_g[:], vs[:].indirect(idx[:]))
+        g_codes, g_scales = quantize("g", g_bf[:].rearrange("p w j -> p (w j)"), Q)
+        o_codes, o_scales = quantize("o", o_g[:].rearrange("p w j -> p (w j)"), G)
+        c1_ps = ps.tile([P, G], F32, name="c1_ps")
+        nc.tensor.matmul_mx(out=c1_ps[:], lhsT=g_codes[:].bitcast(FP8X4), lhsT_scale=g_scales[:],
+                            rhs=o_codes[:].bitcast(FP8X4), rhs_scale=o_scales[:], start=True, stop=True)
+        c0_ps = ps.tile([P, I], F32, name="c0_ps")
+        nc.tensor.matmul_mx(out=c0_ps[:], lhsT=g_codes[:].bitcast(FP8X4), lhsT_scale=g_scales[:],
+                            rhs=vw_g[:].bitcast(FP4X4), rhs_scale=vs_g[:], start=True, stop=True)
+
+        rz = tile("rz", [P, 1], F32)
+        nc.vector.reciprocal(rz[:], z[:])
+        e_sb = tile("e_sb", [P, G], F32)
+        nc.scalar.activation(e_sb[:], c1_ps[:], ACT.Copy, scale=pf_sb[:])
+        pn = tile("pn", [P, I], F32)
+        nc.scalar.activation(pn[:], p_sb[:].rearrange("q t p -> q (t p)"), ACT.Copy, scale=rz[:])
+
+        c_sb = tile("c_sb", [P, PACK, G, PAGE // PACK], F32)
+        nc.vector.tensor_tensor(c_sb[:], c0_ps[:].rearrange("q (g h t) -> q t g h", h=PAGE // PACK, t=PACK),
+                                e_sb[:].unsqueeze(1).unsqueeze(3).broadcast_to([P, PACK, G, PAGE // PACK]), ALU.add)
+        c_flat = c_sb[:].rearrange("q t g h -> q (t g h)")
+        pc = tile("pc", [P, I], F32)
+        mean = tile("mean", [P, 1], F32)
+        nc.vector.scalar_tensor_tensor(pc[:], c_flat, 1.0, pn[:], ALU.mult, ALU.mult, accum_out=mean[:])
+        da = tile("da", [P, I], F32)
+        nc.vector.scalar_tensor_tensor(da[:], c_flat, mean[:], pn[:], ALU.subtract, ALU.mult)
+        da_ps = ps.tile([P, PACK, Q], F32, name="da_ps")
+        for t in range(PACK):
+            nc.tensor.transpose(da_ps[:, t, :], da[:, t * P:(t + 1) * P], ident[:])
+        gs_bf = tile("gs_bf", [P, Q, PACK], BF16)
+        nc.vector.tensor_tensor(gs_bf[:], da_ps[:].rearrange("p t q -> p q t"),
+                                fs_sb[:].unsqueeze(1).broadcast_to([P, Q, PACK]), ALU.mult)
+        gs_codes, gs_scales = quantize("gs", gs_bf[:].rearrange("p w j -> p (w j)"), Q)
+
+        groups = [(0, DT - 1), (DT - 1, DT)]
+        kt_banks = [ps.tile([P, 2, P], F32, name="kt_ps%d" % b) for b in range(2)]
+        for n, (j0, j1) in enumerate(groups):
+            width = (j1 - j0) * P
+            gq_ps = ps.tile([P, width], F32, name="gq_ps%d" % n)
+            for j in range(j0, j1):
+                kt_g = tile("kt_g%d" % j, [P, I], BF16)
+                nc.vector.tensor_copy(kt_g[:], kr[j][:].indirect(idx[:]))
+                words = kt_g[:].bitcast(F32)
+                kt_ps = kt_banks[j % 2]
+                for u in range(2):
+                    nc.tensor.transpose(kt_ps[:, u, :], words[:, u:I // 2:2], ident[:])
+                kt_bf = tile("kt_bf%d" % j, [P, P * PACK], BF16)
+                nc.scalar.copy(kt_bf[:].bitcast(F32).rearrange("p (d u) -> p d u", u=2),
+                               kt_ps[:].rearrange("p u d -> p d u"))
+                kt_codes, kt_scales = quantize("kt%d" % j, kt_bf[:], P)
+                nc.tensor.matmul_mx(out=gq_ps[:, (j - j0) * P:(j - j0 + 1) * P],
+                                    lhsT=gs_codes[:].bitcast(FP8X4), lhsT_scale=gs_scales[:],
+                                    rhs=kt_codes[:].bitcast(FP8X4), rhs_scale=kt_scales[:], start=True, stop=True)
+            y = tile("y%d" % n, [P, width], F32)
+            nc.vector.tensor_tensor(y[:], gq_ps[:], res_sb[:, j0 * P:j1 * P], ALU.add)
+            nc.sync.dma_start(out[:, j0 * P:j1 * P], y[:])

@@ -1,7 +1,6 @@
 from contextlib import ExitStack
 
 import concourse.mybir as mybir
-from concourse.masks import make_identity
 
 D, E, T, I, Q, G, U = 512, 512, 2048, 512, 128, 64, 256
 FLOPS = 2 * Q * (D * I + E * I + E * G + I * D)
@@ -22,6 +21,24 @@ P = 128
 PACK = 4
 DT = D // P
 PAGE = I // G
+KR = 4 * T
+Q_AT = 0
+G_AT = Q_AT + 4 * PACK * Q
+O_AT = G_AT + 4 * PACK * Q
+VS_AT = O_AT + 4 * PACK * U
+WARM_AT = VS_AT + T
+ZERO_AT = WARM_AT + 64
+KR_AT = ZERO_AT + 4 * P
+RES_AT = KR_AT + DT * KR
+KRB_AT = RES_AT + 4 * D
+PSB_AT = KRB_AT + 2 * T - 4 * I - 64
+PF_AT = PSB_AT + 4 * I
+FS_AT = PF_AT + 64
+LATE_END = FS_AT + 64
+Z_AT = LATE_END
+QBF_AT = Z_AT + 2 * I
+PN_AT = QBF_AT + 2 * I
+C_AT = KR_AT
 
 
 def tile_attend_bpageoffsets_q_kernel(tc, query, keys_words, keys_scales, gout, vals_words, vals_scales,
@@ -29,105 +46,133 @@ def tile_attend_bpageoffsets_q_kernel(tc, query, keys_words, keys_scales, gout, 
     nc = tc.nc
     with ExitStack() as ctx:
         sb = ctx.enter_context(tc.tile_pool(name="sb", bufs=1))
+        placed = ctx.enter_context(tc.tile_pool(name="placed", bufs=1))
         ps = ctx.enter_context(tc.psum_pool(name="ps", bufs=1))
 
-        def tile(name, shape, dtype):
-            return sb.tile(shape, dtype, name=name, align_bytes=64)
+        def tile(name, shape, dtype, offset=None):
+            if offset is None:
+                return sb.tile(shape, dtype, name=name, align_bytes=64)
+            return placed.tile(shape, dtype, name=name, align_bytes=64, offset=offset)
 
-        def quantize(name, grouped, words):
-            codes = tile(name + "_codes", [P, words], U32)
+        def quantize(name, grouped, words, offset=None):
+            codes = tile(name + "_codes", [P, words], U32, offset)
             scales = tile(name + "_scales", [P, words], U8)
             nc.vector.quantize_mx(out=codes[:].bitcast(FP8X4), scales=scales[:], in_=grouped)
             return codes, scales
 
         idx = tile("idx", [P, I // 16], U16)
         idx2 = tile("idx2", [P, G // 16], U16)
+        ident = tile("ident", [P, P], F32)
+        warm_out = tile("warm_out", [P, 1], F32)
+        o_bf = tile("o_bf", [P, (PACK + 1) * U], BF16)
         kw = tile("kw", [P, T], U16)
         vw = tile("vw", [P, T], U16)
         ks = tile("ks", [P, T], U8)
-        vs = tile("vs", [P, T], U8)
-        q_raw = tile("q_raw", [P, PACK, Q], F32)
-        g_raw = tile("g_raw", [P, PACK, Q], F32)
-        o_raw = tile("o_raw", [P, PACK * U], F32)
-        pf_sb = tile("pf_sb", [P, 1], F32)
-        fs_sb = tile("fs_sb", [P, PACK], F32)
-        kr = [tile("kr%d" % j, [P, T], F32) for j in range(DT)]
-        res_sb = tile("res_sb", [P, D], F32)
-        ident = tile("ident", [P, P], F32)
-        warm = tile("warm", [P, 1], F32)
-        warm_out = tile("warm_out", [P, 1], F32)
-        o_bf = tile("o_bf", [P, (PACK + 1) * U], BF16)
+        warm = tile("warm", [P, KR_AT // 4], F32, 0)
+        warm_in = warm[:, WARM_AT // 4:WARM_AT // 4 + 1]
 
         nc.vector.memset(ks[:].bitcast(I32), 0)
-        nc.vector.memset(vs[:].bitcast(I32), 0)
-        nc.vector.memset(warm[:], 0.0)
+        nc.vector.memset(warm_in, 0.0)
         nc.vector.memset(o_bf[:, PACK * U:], 0.0)
-        make_identity(nc, ident[:])
+        nc.scalar.activation(warm_out[:], warm_in, ACT.Exp)
 
         nc.sync.dma_start(idx[:], offs)
-        nc.sync.dma_start(kw[:].bitcast(I32), keys_words[0].bitcast(I32))
-        for c in range(4):
-            nc.scalar.dma_start(ks[32 * c:32 * c + 4, :].bitcast(I32), keys_scales[0, 4 * c:4 * c + 4, :].bitcast(I32))
-        nc.scalar.activation(warm_out[:], warm[:], ACT.Exp)
-        nc.sync.dma_start(q_raw[:], query.rearrange("(p j) w -> p j w", j=PACK))
-        nc.sync.dma_start(o_raw[:], pofs.rearrange("(p j) w -> p (j w)", j=PACK))
         nc.sync.dma_start(idx2[:], offs2)
-        nc.sync.dma_start(g_raw[:], gout.rearrange("(p j) w -> p j w", j=PACK))
+        nc.sync.dma_start(kw[:].bitcast(I32), keys_words[0].bitcast(I32))
         nc.sync.dma_start(vw[:].bitcast(I32), vals_words[0].bitcast(I32))
         for c in range(4):
-            nc.scalar.dma_start(vs[32 * c:32 * c + 4, :].bitcast(I32), vals_scales[0, 4 * c:4 * c + 4, :].bitcast(I32))
-        for j in range(DT):
+            nc.sync.dma_start(ks[32 * c:32 * c + 4, :].bitcast(I32), keys_scales[0, 4 * c:4 * c + 4, :].bitcast(I32))
+
+        q_raw = tile("q_raw", [P, PACK, Q], F32, Q_AT)
+        nc.sync.dma_start(q_raw[:], query.rearrange("(p j) w -> p j w", j=PACK))
+        g_raw = tile("g_raw", [P, PACK, Q], F32, G_AT)
+        nc.sync.dma_start(g_raw[:], gout.rearrange("(p j) w -> p j w", j=PACK))
+        o_raw = tile("o_raw", [P, PACK * U], F32, O_AT)
+        nc.sync.dma_start(o_raw[:], pofs.rearrange("(p j) w -> p (j w)", j=PACK))
+        vs = tile("vs", [P, T], U8, VS_AT)
+        nc.gpsimd.memset(vs[:].bitcast(I32), 0)
+        for c in range(4):
+            nc.sync.dma_start(vs[32 * c:32 * c + 4, :].bitcast(I32), vals_scales[0, 4 * c:4 * c + 4, :].bitcast(I32))
+
+        late = tile("late", [P, (LATE_END - ZERO_AT) // 4], F32, ZERO_AT)
+        nc.gpsimd.memset(late[:, :P], 0.0)
+        nc.gpsimd.affine_select(out=ident[:], in_=late[:, :P], compare_op=ALU.not_equal, fill=1.0, base=0,
+                                pattern=[[-1, P]], channel_multiplier=1)
+        kr = {}
+
+        def load_rows(j):
+            kr[j] = tile("kr%d" % j, [P, T], F32, KR_AT + j * KR)
             nc.sync.dma_start(kr[j][:], keyrows[j * P:(j + 1) * P, :])
+
+        load_rows(0)
+        pf_sb = tile("pf_sb", [P, 1], F32, PF_AT)
+        nc.sync.dma_start(pf_sb[:], pf)
+        fs_sb = tile("fs_sb", [P, PACK], F32, FS_AT)
+        nc.sync.dma_start(fs_sb[:], fs.rearrange("o (p t) -> (o p) t", t=PACK))
+        for j in (2, 1, 3):
+            load_rows(j)
+        res_sb = tile("res_sb", [P, D], F32, RES_AT)
         nc.sync.dma_start(res_sb[:], res)
-        nc.gpsimd.dma_start(pf_sb[:], pf)
-        nc.gpsimd.dma_start(fs_sb[:], fs.rearrange("o (p t) -> (o p) t", t=PACK))
+
+        kt_g = {}
+        kt_bf = [tile("kt_bf%d" % h, [P, 2, P * PACK], BF16) for h in range(DT // 2)]
+
+        def turn(j, bank):
+            kt_ps = ps.tile([P, 2, P], F32, name="kt_ps%d" % j, tag=bank)
+            words = kt_g[j][:].bitcast(F32)
+            for u in range(2):
+                nc.tensor.transpose(kt_ps[:, u, :], words[:, u:I // 2:2], ident[:])
+            nc.scalar.copy(kt_bf[j // 2][:, j % 2, :].bitcast(F32).rearrange("p (d u) -> p d u", u=2),
+                           kt_ps[:].rearrange("p u d -> p d u"))
 
         kw_g = tile("kw_g", [P, I], U16)
         ks_g = tile("ks_g", [P, I], U8)
-        nc.vector.tensor_copy(kw_g[:], kw[:].indirect(idx[:]))
-        q_bf = tile("q_bf", [P, Q, PACK], BF16)
+        vs_g = tile("vs_g", [P, I], U8)
+        q_bf = tile("q_bf", [P, Q, PACK], BF16, QBF_AT)
+        g_bf = tile("g_bf", [P, Q, PACK], BF16)
         nc.scalar.copy(q_bf[:], q_raw[:].rearrange("p j w -> p w j"))
+        nc.scalar.copy(g_bf[:], g_raw[:].rearrange("p j w -> p w j"))
+        nc.vector.tensor_copy(kw_g[:], kw[:].indirect(idx[:]))
         nc.vector.tensor_copy(ks_g[:], ks[:].indirect(idx[:]))
         q_codes, q_scales = quantize("q", q_bf[:].rearrange("p w j -> p (w j)"), Q)
-        a_ps = ps.tile([P, I], F32, name="a_ps")
+        a_ps = ps.tile([P, I], F32, name="a_ps", tag="a")
         nc.tensor.matmul_mx(out=a_ps[:], lhsT=q_codes[:].bitcast(FP8X4), lhsT_scale=q_scales[:],
                             rhs=kw_g[:].bitcast(FP4X4), rhs_scale=ks_g[:], start=True, stop=True)
+        vw_g = tile("vw_g", [P, I], U16, QBF_AT)
+        nc.vector.tensor_copy(vw_g[:], vw[:].indirect(idx[:]))
+        neg_max = tile("neg_max", [P, 1], F32)
+        nc.vector.tensor_reduce(neg_max[:], a_ps[:], AX.X, ALU.max, negate=True)
+        nc.vector.tensor_copy(vs_g[:], vs[:].indirect(idx[:]))
+        g_codes, g_scales = quantize("g", g_bf[:].rearrange("p w j -> p (w j)"), Q)
+        c0_ps = ps.tile([P, I], F32, name="c0_ps")
+        nc.tensor.matmul_mx(out=c0_ps[:], lhsT=g_codes[:].bitcast(FP8X4), lhsT_scale=g_scales[:],
+                            rhs=vw_g[:].bitcast(FP4X4), rhs_scale=vs_g[:], start=True, stop=True)
 
         nc.scalar.copy(o_bf[:, :PACK * U], o_raw[:])
         o_g = tile("o_g", [P, G, PACK], BF16)
         for t in range(PACK):
             nc.scalar.activation(o_g[:, :, t], o_bf[:, t * U:(t + 2) * U].indirect(idx2[:]), ACT.Copy)
-        g_bf = tile("g_bf", [P, Q, PACK], BF16)
-        nc.scalar.copy(g_bf[:], g_raw[:].rearrange("p j w -> p w j"))
 
-        neg_max = tile("neg_max", [P, 1], F32)
-        nc.vector.tensor_reduce(neg_max[:], a_ps[:], AX.X, ALU.max, negate=True)
-        p_sb = tile("p_sb", [P, PACK, P], F32)
-        z = tile("z", [P, 1], F32)
+        p_sb = tile("p_sb", [P, PACK, P], F32, PSB_AT)
+        z = tile("z", [P, 1], F32, Z_AT)
         nc.scalar.activation(p_sb[:], a_ps[:].rearrange("q (p t) -> q t p", t=PACK), ACT.Exp,
                              bias=neg_max[:], accum_out=z[:])
 
-        vw_g = tile("vw_g", [P, I], U16)
-        vs_g = tile("vs_g", [P, I], U8)
-        nc.vector.tensor_copy(vw_g[:], vw[:].indirect(idx[:]))
-        nc.vector.tensor_copy(vs_g[:], vs[:].indirect(idx[:]))
-        g_codes, g_scales = quantize("g", g_bf[:].rearrange("p w j -> p (w j)"), Q)
         o_codes, o_scales = quantize("o", o_g[:].rearrange("p w j -> p (w j)"), G)
         c1_ps = ps.tile([P, G], F32, name="c1_ps")
         nc.tensor.matmul_mx(out=c1_ps[:], lhsT=g_codes[:].bitcast(FP8X4), lhsT_scale=g_scales[:],
                             rhs=o_codes[:].bitcast(FP8X4), rhs_scale=o_scales[:], start=True, stop=True)
-        c0_ps = ps.tile([P, I], F32, name="c0_ps")
-        nc.tensor.matmul_mx(out=c0_ps[:], lhsT=g_codes[:].bitcast(FP8X4), lhsT_scale=g_scales[:],
-                            rhs=vw_g[:].bitcast(FP4X4), rhs_scale=vs_g[:], start=True, stop=True)
-
-        rz = tile("rz", [P, 1], F32)
+        rz = tile("rz", [P, 1], F32, VS_AT)
         nc.vector.reciprocal(rz[:], z[:])
+        kt_g[0] = tile("kt_g0", [P, I], BF16, Z_AT)
+        nc.vector.tensor_copy(kt_g[0][:], kr[0][:].indirect(idx[:]))
         e_sb = tile("e_sb", [P, G], F32)
         nc.scalar.activation(e_sb[:], c1_ps[:], ACT.Copy, scale=pf_sb[:])
-        pn = tile("pn", [P, I], F32)
+        pn = tile("pn", [P, I], F32, PN_AT)
         nc.scalar.activation(pn[:], p_sb[:].rearrange("q t p -> q (t p)"), ACT.Copy, scale=rz[:])
+        turn(0, "kt_a")
 
-        c_sb = tile("c_sb", [P, PACK, G, PAGE // PACK], F32)
+        c_sb = tile("c_sb", [P, PACK, G, PAGE // PACK], F32, C_AT)
         nc.vector.tensor_tensor(c_sb[:], c0_ps[:].rearrange("q (g h t) -> q t g h", h=PAGE // PACK, t=PACK),
                                 e_sb[:].unsqueeze(1).unsqueeze(3).broadcast_to([P, PACK, G, PAGE // PACK]), ALU.add)
         c_flat = c_sb[:].rearrange("q t g h -> q (t g h)")
@@ -136,33 +181,34 @@ def tile_attend_bpageoffsets_q_kernel(tc, query, keys_words, keys_scales, gout, 
         nc.vector.scalar_tensor_tensor(pc[:], c_flat, 1.0, pn[:], ALU.mult, ALU.mult, accum_out=mean[:])
         da = tile("da", [P, I], F32)
         nc.vector.scalar_tensor_tensor(da[:], c_flat, mean[:], pn[:], ALU.subtract, ALU.mult)
+
+        kr2_bf = tile("kr2_bf", [P, T], BF16, KRB_AT)
+        kt_g[2] = tile("kt_g2", [P, I], BF16, PN_AT)
+        kt_g[1] = tile("kt_g1", [P, I], BF16, C_AT)
+        nc.scalar.copy(kr2_bf[:], kr[2][:])
+        nc.scalar.activation(kt_g[2][:], kr2_bf[:].indirect(idx[:]), ACT.Copy)
+        nc.vector.tensor_copy(kt_g[1][:], kr[1][:].indirect(idx[:]))
+        kt_g[3] = tile("kt_g3", [P, I], BF16, PN_AT + 2 * I)
+        nc.vector.tensor_copy(kt_g[3][:], kr[3][:].indirect(idx[:]))
+
         da_ps = ps.tile([P, PACK, Q], F32, name="da_ps")
         for t in range(PACK):
             nc.tensor.transpose(da_ps[:, t, :], da[:, t * P:(t + 1) * P], ident[:])
-        gs_bf = tile("gs_bf", [P, Q, PACK], BF16)
+        gs_bf = tile("gs_bf", [P, Q, PACK], BF16, KR_AT + 3 * KR + KR // 2)
         nc.vector.tensor_tensor(gs_bf[:], da_ps[:].rearrange("p t q -> p q t"),
                                 fs_sb[:].unsqueeze(1).broadcast_to([P, Q, PACK]), ALU.mult)
+        turn(1, "kt_b")
+        turn(2, "a")
+        turn(3, "kt_a")
         gs_codes, gs_scales = quantize("gs", gs_bf[:].rearrange("p w j -> p (w j)"), Q)
 
-        groups = [(0, DT - 1), (DT - 1, DT)]
-        kt_banks = [ps.tile([P, 2, P], F32, name="kt_ps%d" % b) for b in range(2)]
-        for n, (j0, j1) in enumerate(groups):
-            width = (j1 - j0) * P
-            gq_ps = ps.tile([P, width], F32, name="gq_ps%d" % n)
-            for j in range(j0, j1):
-                kt_g = tile("kt_g%d" % j, [P, I], BF16)
-                nc.vector.tensor_copy(kt_g[:], kr[j][:].indirect(idx[:]))
-                words = kt_g[:].bitcast(F32)
-                kt_ps = kt_banks[j % 2]
-                for u in range(2):
-                    nc.tensor.transpose(kt_ps[:, u, :], words[:, u:I // 2:2], ident[:])
-                kt_bf = tile("kt_bf%d" % j, [P, P * PACK], BF16)
-                nc.scalar.copy(kt_bf[:].bitcast(F32).rearrange("p (d u) -> p d u", u=2),
-                               kt_ps[:].rearrange("p u d -> p d u"))
-                kt_codes, kt_scales = quantize("kt%d" % j, kt_bf[:], P)
-                nc.tensor.matmul_mx(out=gq_ps[:, (j - j0) * P:(j - j0 + 1) * P],
-                                    lhsT=gs_codes[:].bitcast(FP8X4), lhsT_scale=gs_scales[:],
-                                    rhs=kt_codes[:].bitcast(FP8X4), rhs_scale=kt_scales[:], start=True, stop=True)
-            y = tile("y%d" % n, [P, width], F32)
-            nc.vector.tensor_tensor(y[:], gq_ps[:], res_sb[:, j0 * P:j1 * P], ALU.add)
-            nc.sync.dma_start(out[:, j0 * P:j1 * P], y[:])
+        for h in range(DT // 2):
+            cols = slice(2 * P * h, 2 * P * (h + 1))
+            kt_codes, kt_scales = quantize("kt%d" % h, kt_bf[h][:].rearrange("p a w -> p (a w)"), 2 * P,
+                                           KR_AT + 3 * KR + (h + 1) * 4 * 2 * P)
+            gq_ps = ps.tile([P, 2 * P], F32, name="gq_ps%d" % h)
+            nc.tensor.matmul_mx(out=gq_ps[:], lhsT=gs_codes[:].bitcast(FP8X4), lhsT_scale=gs_scales[:],
+                                rhs=kt_codes[:].bitcast(FP8X4), rhs_scale=kt_scales[:], start=True, stop=True)
+            y = tile("y%d" % h, [P, 2 * P], F32)
+            nc.vector.tensor_tensor(y[:], gq_ps[:], res_sb[:, cols], ALU.add)
+            nc.sync.dma_start(out[:, cols], y[:])

@@ -38,6 +38,7 @@ LATE_END = FS_AT + 64
 Z_AT = LATE_END
 QBF_AT = Z_AT + 2 * I
 PN_AT = QBF_AT + 2 * I
+PC_AT = PN_AT + 4 * I
 C_AT = KR_AT
 
 
@@ -64,7 +65,6 @@ def tile_attend_bpageoffsets_q_kernel(tc, query, keys_words, keys_scales, gout, 
         idx2 = tile("idx2", [P, G // 16], U16)
         ident = tile("ident", [P, P], F32)
         warm_out = tile("warm_out", [P, 1], F32)
-        o_bf = tile("o_bf", [P, (PACK + 1) * U], BF16)
         kw = tile("kw", [P, T], U16)
         vw = tile("vw", [P, T], U16)
         ks = tile("ks", [P, T], U8)
@@ -73,7 +73,6 @@ def tile_attend_bpageoffsets_q_kernel(tc, query, keys_words, keys_scales, gout, 
 
         nc.vector.memset(ks[:].bitcast(I32), 0)
         nc.vector.memset(warm_in, 0.0)
-        nc.vector.memset(o_bf[:, PACK * U:], 0.0)
         nc.scalar.activation(warm_out[:], warm_in, ACT.Exp)
 
         nc.sync.dma_start(idx[:], offs)
@@ -90,7 +89,7 @@ def tile_attend_bpageoffsets_q_kernel(tc, query, keys_words, keys_scales, gout, 
         o_raw = tile("o_raw", [P, PACK * U], F32, O_AT)
         nc.sync.dma_start(o_raw[:], pofs.rearrange("(p j) w -> p (j w)", j=PACK))
         vs = tile("vs", [P, T], U8, VS_AT)
-        nc.gpsimd.memset(vs[:].bitcast(I32), 0)
+        nc.vector.memset(vs[:].bitcast(I32), 0)
         for c in range(4):
             nc.sync.dma_start(vs[32 * c:32 * c + 4, :].bitcast(I32), vals_scales[0, 4 * c:4 * c + 4, :].bitcast(I32))
 
@@ -115,15 +114,18 @@ def tile_attend_bpageoffsets_q_kernel(tc, query, keys_words, keys_scales, gout, 
         nc.sync.dma_start(res_sb[:], res)
 
         kt_g = {}
-        kt_bf = [tile("kt_bf%d" % h, [P, 2, P * PACK], BF16) for h in range(DT // 2)]
+        kt_bf = tile("kt_bf", [P, DT * P * PACK], BF16)
 
         def turn(j, bank):
             kt_ps = ps.tile([P, 2, P], F32, name="kt_ps%d" % j, tag=bank)
             words = kt_g[j][:].bitcast(F32)
             for u in range(2):
                 nc.tensor.transpose(kt_ps[:, u, :], words[:, u:I // 2:2], ident[:])
-            nc.scalar.copy(kt_bf[j // 2][:, j % 2, :].bitcast(F32).rearrange("p (d u) -> p d u", u=2),
+            nc.scalar.copy(kt_bf[:, j * P * PACK:(j + 1) * P * PACK].bitcast(F32).rearrange("p (d u) -> p d u", u=2),
                            kt_ps[:].rearrange("p u d -> p d u"))
+
+        def quantize_rows(j0, j1, offset=None):
+            return quantize("kt%d" % j0, kt_bf[:, j0 * P * PACK:j1 * P * PACK], (j1 - j0) * P, offset)
 
         kw_g = tile("kw_g", [P, I], U16)
         ks_g = tile("ks_g", [P, I], U8)
@@ -148,10 +150,13 @@ def tile_attend_bpageoffsets_q_kernel(tc, query, keys_words, keys_scales, gout, 
         nc.tensor.matmul_mx(out=c0_ps[:], lhsT=g_codes[:].bitcast(FP8X4), lhsT_scale=g_scales[:],
                             rhs=vw_g[:].bitcast(FP4X4), rhs_scale=vs_g[:], start=True, stop=True)
 
-        nc.scalar.copy(o_bf[:, :PACK * U], o_raw[:])
-        o_g = tile("o_g", [P, G, PACK], BF16)
+        o_planes = tile("o_planes", [P, PACK, G], BF16)
         for t in range(PACK):
-            nc.scalar.activation(o_g[:, :, t], o_bf[:, t * U:(t + 2) * U].indirect(idx2[:]), ACT.Copy)
+            o_bf = tile("o_bf%d" % t, [P, U], BF16)
+            nc.scalar.activation(o_bf[:], o_raw[:, t * U:(t + 1) * U], ACT.Copy)
+            nc.scalar.activation(o_planes[:, t, :], o_bf[:].indirect(idx2[:]), ACT.Copy)
+        o_g = tile("o_g", [P, G, PACK], BF16)
+        nc.scalar.copy(o_g[:], o_planes[:].rearrange("p t g -> p g t"))
 
         p_sb = tile("p_sb", [P, PACK, P], F32, PSB_AT)
         z = tile("z", [P, 1], F32, Z_AT)
@@ -176,19 +181,20 @@ def tile_attend_bpageoffsets_q_kernel(tc, query, keys_words, keys_scales, gout, 
         nc.vector.tensor_tensor(c_sb[:], c0_ps[:].rearrange("q (g h t) -> q t g h", h=PAGE // PACK, t=PACK),
                                 e_sb[:].unsqueeze(1).unsqueeze(3).broadcast_to([P, PACK, G, PAGE // PACK]), ALU.add)
         c_flat = c_sb[:].rearrange("q t g h -> q (t g h)")
-        pc = tile("pc", [P, I], F32)
+        pc = tile("pc", [P, I], F32, PC_AT)
         mean = tile("mean", [P, 1], F32)
         nc.vector.scalar_tensor_tensor(pc[:], c_flat, 1.0, pn[:], ALU.mult, ALU.mult, accum_out=mean[:])
+        kt_q = {0: quantize_rows(0, 1, PC_AT)}
         da = tile("da", [P, I], F32)
         nc.vector.scalar_tensor_tensor(da[:], c_flat, mean[:], pn[:], ALU.subtract, ALU.mult)
 
         kr2_bf = tile("kr2_bf", [P, T], BF16, KRB_AT)
-        kt_g[2] = tile("kt_g2", [P, I], BF16, PN_AT)
+        kt_g[2] = tile("kt_g2", [P, I], BF16)
         kt_g[1] = tile("kt_g1", [P, I], BF16, C_AT)
         nc.scalar.copy(kr2_bf[:], kr[2][:])
         nc.scalar.activation(kt_g[2][:], kr2_bf[:].indirect(idx[:]), ACT.Copy)
         nc.vector.tensor_copy(kt_g[1][:], kr[1][:].indirect(idx[:]))
-        kt_g[3] = tile("kt_g3", [P, I], BF16, PN_AT + 2 * I)
+        kt_g[3] = tile("kt_g3", [P, I], BF16, PN_AT)
         nc.vector.tensor_copy(kt_g[3][:], kr[3][:].indirect(idx[:]))
 
         da_ps = ps.tile([P, PACK, Q], F32, name="da_ps")
@@ -200,15 +206,20 @@ def tile_attend_bpageoffsets_q_kernel(tc, query, keys_words, keys_scales, gout, 
         turn(1, "kt_b")
         turn(2, "a")
         turn(3, "kt_a")
+        kt_q[1] = quantize_rows(1, 3, KR_AT + 3 * KR)
         gs_codes, gs_scales = quantize("gs", gs_bf[:].rearrange("p w j -> p (w j)"), Q)
 
-        for h in range(DT // 2):
-            cols = slice(2 * P * h, 2 * P * (h + 1))
-            kt_codes, kt_scales = quantize("kt%d" % h, kt_bf[h][:].rearrange("p a w -> p (a w)"), 2 * P,
-                                           KR_AT + 3 * KR + (h + 1) * 4 * 2 * P)
-            gq_ps = ps.tile([P, 2 * P], F32, name="gq_ps%d" % h)
-            nc.tensor.matmul_mx(out=gq_ps[:], lhsT=gs_codes[:].bitcast(FP8X4), lhsT_scale=gs_scales[:],
-                                rhs=kt_codes[:].bitcast(FP8X4), rhs_scale=kt_scales[:], start=True, stop=True)
-            y = tile("y%d" % h, [P, 2 * P], F32)
+        kt_q[3] = quantize_rows(3, 4)
+
+        for name, spans in (("head", ((0, 1), (1, 3))), ("last", ((3, 4),))):
+            cols = slice(spans[0][0] * P, spans[-1][1] * P)
+            width = cols.stop - cols.start
+            gq_ps = ps.tile([P, width], F32, name="gq_ps_" + name)
+            for j0, j1 in spans:
+                kt_codes, kt_scales = kt_q[j0]
+                nc.tensor.matmul_mx(out=gq_ps[:, j0 * P - cols.start:j1 * P - cols.start],
+                                    lhsT=gs_codes[:].bitcast(FP8X4), lhsT_scale=gs_scales[:],
+                                    rhs=kt_codes[:].bitcast(FP8X4), rhs_scale=kt_scales[:], start=True, stop=True)
+            y = tile("y_" + name, [P, width], F32)
             nc.vector.tensor_tensor(y[:], gq_ps[:], res_sb[:, cols], ALU.add)
             nc.sync.dma_start(out[:, cols], y[:])

from contextlib import ExitStack

import concourse.mybir as mybir

D, E, T, I, Q, G, U = 512, 512, 2048, 512, 128, 64, 256
FLOPS = 2 * Q * (D * I + E * I + E * G + I * D)

F32 = mybir.dt.float32
BF16 = mybir.dt.bfloat16
I32 = mybir.dt.int32
U32 = mybir.dt.uint32
U16 = mybir.dt.uint16
U8 = mybir.dt.uint8
FP8X4 = mybir.dt.float8_e4m3fn_x4
FP4X4 = mybir.dt.float4_e2m1fn_x4
ACT = mybir.ActivationFunctionType
ALU = mybir.AluOpType
AX = mybir.AxisListType

P = 128
PACK = 4
DT = D // P
PAGE = I // G
KR = 4 * T
Q_AT = 0
G_AT = Q_AT + 4 * PACK * Q
O_AT = G_AT + 4 * PACK * Q
VS_AT = O_AT + 4 * PACK * U
WARM_AT = VS_AT + T
ZERO_AT = WARM_AT + 64
KR_AT = ZERO_AT + 4 * P
RES_AT = KR_AT + DT * KR
KRB_AT = RES_AT + 4 * D
PSB_AT = KRB_AT + 2 * T - 4 * I - 64
PF_AT = PSB_AT + 4 * I
FS_AT = PF_AT + 64
LATE_END = FS_AT + 64
Z_AT = LATE_END
QBF_AT = Z_AT + 2 * I
PN_AT = QBF_AT + 2 * I
PC_AT = PN_AT + 4 * I
C_AT = KR_AT


def tile_attend_bpageoffsets_q_kernel(tc, query, keys_words, keys_scales, gout, vals_words, vals_scales,
                                       pofs, pf, fs, keyrows, res, offs, offs2, out):
    nc = tc.nc
    with ExitStack() as ctx:
        sb = ctx.enter_context(tc.tile_pool(name="sb", bufs=1))
        placed = ctx.enter_context(tc.tile_pool(name="placed", bufs=1))
        ps = ctx.enter_context(tc.psum_pool(name="ps", bufs=1))

        def tile(name, shape, dtype, offset=None):
            if offset is None:
                return sb.tile(shape, dtype, name=name, align_bytes=64)
            return placed.tile(shape, dtype, name=name, align_bytes=64, offset=offset)

        def quantize(name, grouped, words, offset=None):
            codes = tile(name + "_codes", [P, words], U32, offset)
            scales = tile(name + "_scales", [P, words], U8)
            nc.vector.quantize_mx(out=codes[:].bitcast(FP8X4), scales=scales[:], in_=grouped)
            return codes, scales

        idx = tile("idx", [P, I // 16], U16)
        idx2 = tile("idx2", [P, G // 16], U16)
        ident = tile("ident", [P, P], F32)
        warm_out = tile("warm_out", [P, 1], F32)
        kw = tile("kw", [P, T], U16)
        vw = tile("vw", [P, T], U16)
        ks = tile("ks", [P, T], U8)
        warm = tile("warm", [P, KR_AT // 4], F32, 0)
        warm_in = warm[:, WARM_AT // 4:WARM_AT // 4 + 1]

        nc.vector.memset(ks[:].bitcast(I32), 0)
        nc.vector.memset(warm_in, 0.0)
        nc.scalar.activation(warm_out[:], warm_in, ACT.Exp)

        nc.sync.dma_start(idx[:], offs)
        nc.sync.dma_start(idx2[:], offs2)
        nc.sync.dma_start(kw[:].bitcast(I32), keys_words[0].bitcast(I32))
        nc.sync.dma_start(vw[:].bitcast(I32), vals_words[0].bitcast(I32))
        for c in range(4):
            nc.sync.dma_start(ks[32 * c:32 * c + 4, :].bitcast(I32), keys_scales[0, 4 * c:4 * c + 4, :].bitcast(I32))

        q_raw = tile("q_raw", [P, PACK, Q], F32, Q_AT)
        nc.sync.dma_start(q_raw[:], query.rearrange("(p j) w -> p j w", j=PACK))
        g_raw = tile("g_raw", [P, PACK, Q], F32, G_AT)
        nc.sync.dma_start(g_raw[:], gout.rearrange("(p j) w -> p j w", j=PACK))
        o_raw = tile("o_raw", [P, PACK * U], F32, O_AT)
        nc.sync.dma_start(o_raw[:], pofs.rearrange("(p j) w -> p (j w)", j=PACK))
        vs = tile("vs", [P, T], U8, VS_AT)
        nc.vector.memset(vs[:].bitcast(I32), 0)
        for c in range(4):
            nc.sync.dma_start(vs[32 * c:32 * c + 4, :].bitcast(I32), vals_scales[0, 4 * c:4 * c + 4, :].bitcast(I32))

        late = tile("late", [P, (LATE_END - ZERO_AT) // 4], F32, ZERO_AT)
        nc.gpsimd.memset(late[:, :P], 0.0)
        nc.gpsimd.affine_select(out=ident[:], in_=late[:, :P], compare_op=ALU.not_equal, fill=1.0, base=0,
                                pattern=[[-1, P]], channel_multiplier=1)
        kr = {}

        def load_rows(j):
            kr[j] = tile("kr%d" % j, [P, T], F32, KR_AT + j * KR)
            nc.sync.dma_start(kr[j][:], keyrows[j * P:(j + 1) * P, :])

        load_rows(0)
        pf_sb = tile("pf_sb", [P, 1], F32, PF_AT)
        nc.sync.dma_start(pf_sb[:], pf)
        fs_sb = tile("fs_sb", [P, PACK], F32, FS_AT)
        nc.sync.dma_start(fs_sb[:], fs.rearrange("o (p t) -> (o p) t", t=PACK))
        for j in (2, 1, 3):
            load_rows(j)
        res_sb = tile("res_sb", [P, D], F32, RES_AT)
        nc.sync.dma_start(res_sb[:], res)

        kt_g = {}
        kt_bf = tile("kt_bf", [P, DT * P * PACK], BF16)

        def turn(j, bank):
            kt_ps = ps.tile([P, 2, P], F32, name="kt_ps%d" % j, tag=bank)
            words = kt_g[j][:].bitcast(F32)
            for u in range(2):
                nc.tensor.transpose(kt_ps[:, u, :], words[:, u:I // 2:2], ident[:])
            nc.scalar.copy(kt_bf[:, j * P * PACK:(j + 1) * P * PACK].bitcast(F32).rearrange("p (d u) -> p d u", u=2),
                           kt_ps[:].rearrange("p u d -> p d u"))

        def quantize_rows(j0, j1, offset=None):
            return quantize("kt%d" % j0, kt_bf[:, j0 * P * PACK:j1 * P * PACK], (j1 - j0) * P, offset)

        kw_g = tile("kw_g", [P, I], U16)
        ks_g = tile("ks_g", [P, I], U8)
        vs_g = tile("vs_g", [P, I], U8)
        q_bf = tile("q_bf", [P, Q, PACK], BF16, QBF_AT)
        g_bf = tile("g_bf", [P, Q, PACK], BF16)
        nc.scalar.copy(q_bf[:], q_raw[:].rearrange("p j w -> p w j"))
        nc.scalar.copy(g_bf[:], g_raw[:].rearrange("p j w -> p w j"))
        nc.vector.tensor_copy(kw_g[:], kw[:].indirect(idx[:]))
        nc.vector.tensor_copy(ks_g[:], ks[:].indirect(idx[:]))
        q_codes, q_scales = quantize("q", q_bf[:].rearrange("p w j -> p (w j)"), Q)
        a_ps = ps.tile([P, I], F32, name="a_ps", tag="a")
        nc.tensor.matmul_mx(out=a_ps[:], lhsT=q_codes[:].bitcast(FP8X4), lhsT_scale=q_scales[:],
                            rhs=kw_g[:].bitcast(FP4X4), rhs_scale=ks_g[:], start=True, stop=True)
        vw_g = tile("vw_g", [P, I], U16, QBF_AT)
        nc.vector.tensor_copy(vw_g[:], vw[:].indirect(idx[:]))
        neg_max = tile("neg_max", [P, 1], F32)
        nc.vector.tensor_reduce(neg_max[:], a_ps[:], AX.X, ALU.max, negate=True)
        nc.vector.tensor_copy(vs_g[:], vs[:].indirect(idx[:]))
        g_codes, g_scales = quantize("g", g_bf[:].rearrange("p w j -> p (w j)"), Q)
        c0_ps = ps.tile([P, I], F32, name="c0_ps")
        nc.tensor.matmul_mx(out=c0_ps[:], lhsT=g_codes[:].bitcast(FP8X4), lhsT_scale=g_scales[:],
                            rhs=vw_g[:].bitcast(FP4X4), rhs_scale=vs_g[:], start=True, stop=True)

        o_planes = tile("o_planes", [P, PACK, G], BF16)
        for t in range(PACK):
            o_bf = tile("o_bf%d" % t, [P, U], BF16)
            nc.scalar.activation(o_bf[:], o_raw[:, t * U:(t + 1) * U], ACT.Copy)
            nc.scalar.activation(o_planes[:, t, :], o_bf[:].indirect(idx2[:]), ACT.Copy)
        o_g = tile("o_g", [P, G, PACK], BF16)
        nc.scalar.copy(o_g[:], o_planes[:].rearrange("p t g -> p g t"))

        p_sb = tile("p_sb", [P, PACK, P], F32, PSB_AT)
        z = tile("z", [P, 1], F32, Z_AT)
        nc.scalar.activation(p_sb[:], a_ps[:].rearrange("q (p t) -> q t p", t=PACK), ACT.Exp,
                             bias=neg_max[:], accum_out=z[:])

        o_codes, o_scales = quantize("o", o_g[:].rearrange("p w j -> p (w j)"), G)
        c1_ps = ps.tile([P, G], F32, name="c1_ps")
        nc.tensor.matmul_mx(out=c1_ps[:], lhsT=g_codes[:].bitcast(FP8X4), lhsT_scale=g_scales[:],
                            rhs=o_codes[:].bitcast(FP8X4), rhs_scale=o_scales[:], start=True, stop=True)
        rz = tile("rz", [P, 1], F32, VS_AT)
        nc.vector.reciprocal(rz[:], z[:])
        kt_g[0] = tile("kt_g0", [P, I], BF16, Z_AT)
        nc.vector.tensor_copy(kt_g[0][:], kr[0][:].indirect(idx[:]))
        e_sb = tile("e_sb", [P, G], F32)
        nc.scalar.activation(e_sb[:], c1_ps[:], ACT.Copy, scale=pf_sb[:])
        pn = tile("pn", [P, I], F32, PN_AT)
        nc.scalar.activation(pn[:], p_sb[:].rearrange("q t p -> q (t p)"), ACT.Copy, scale=rz[:])
        turn(0, "kt_a")

        c_sb = tile("c_sb", [P, PACK, G, PAGE // PACK], F32, C_AT)
        nc.vector.tensor_tensor(c_sb[:], c0_ps[:].rearrange("q (g h t) -> q t g h", h=PAGE // PACK, t=PACK),
                                e_sb[:].unsqueeze(1).unsqueeze(3).broadcast_to([P, PACK, G, PAGE // PACK]), ALU.add)
        c_flat = c_sb[:].rearrange("q t g h -> q (t g h)")
        pc = tile("pc", [P, I], F32, PC_AT)
        mean = tile("mean", [P, 1], F32)
        nc.vector.scalar_tensor_tensor(pc[:], c_flat, 1.0, pn[:], ALU.mult, ALU.mult, accum_out=mean[:])
        kt_q = {0: quantize_rows(0, 1, PC_AT)}
        da = tile("da", [P, I], F32)
        nc.vector.scalar_tensor_tensor(da[:], c_flat, mean[:], pn[:], ALU.subtract, ALU.mult)

        kr2_bf = tile("kr2_bf", [P, T], BF16, KRB_AT)
        kt_g[2] = tile("kt_g2", [P, I], BF16)
        kt_g[1] = tile("kt_g1", [P, I], BF16, C_AT)
        nc.scalar.copy(kr2_bf[:], kr[2][:])
        nc.scalar.activation(kt_g[2][:], kr2_bf[:].indirect(idx[:]), ACT.Copy)
        nc.vector.tensor_copy(kt_g[1][:], kr[1][:].indirect(idx[:]))
        kt_g[3] = tile("kt_g3", [P, I], BF16, PN_AT)
        nc.vector.tensor_copy(kt_g[3][:], kr[3][:].indirect(idx[:]))

        da_ps = ps.tile([P, PACK, Q], F32, name="da_ps")
        for t in range(PACK):
            nc.tensor.transpose(da_ps[:, t, :], da[:, t * P:(t + 1) * P], ident[:])
        gs_bf = tile("gs_bf", [P, Q, PACK], BF16, KR_AT + 3 * KR + KR // 2)
        nc.vector.tensor_tensor(gs_bf[:], da_ps[:].rearrange("p t q -> p q t"),
                                fs_sb[:].unsqueeze(1).broadcast_to([P, Q, PACK]), ALU.mult)
        turn(1, "kt_b")
        turn(2, "a")
        turn(3, "kt_a")
        kt_q[1] = quantize_rows(1, 3, KR_AT + 3 * KR)
        gs_codes, gs_scales = quantize("gs", gs_bf[:].rearrange("p w j -> p (w j)"), Q)

        kt_q[3] = quantize_rows(3, 4)

        for name, spans in (("head", ((0, 1), (1, 3))), ("last", ((3, 4),))):
            cols = slice(spans[0][0] * P, spans[-1][1] * P)
            width = cols.stop - cols.start
            gq_ps = ps.tile([P, width], F32, name="gq_ps_" + name)
            for j0, j1 in spans:
                kt_codes, kt_scales = kt_q[j0]
                nc.tensor.matmul_mx(out=gq_ps[:, j0 * P - cols.start:j1 * P - cols.start],
                                    lhsT=gs_codes[:].bitcast(FP8X4), lhsT_scale=gs_scales[:],
                                    rhs=kt_codes[:].bitcast(FP8X4), rhs_scale=kt_scales[:], start=True, stop=True)
            y = tile("y_" + name, [P, width], F32)
            nc.vector.tensor_tensor(y[:], gq_ps[:], res_sb[:, cols], ALU.add)
            nc.sync.dma_start(out[:, cols], y[:])
